import numpy as np
import ml_dtypes


def mxq(x, axis, fmt="e4m3"):
    dtype, down = {"e4m3": (ml_dtypes.float8_e4m3fn, 7), "e5m2": (ml_dtypes.float8_e5m2, 14)}[fmt]
    v = np.moveaxis(np.asarray(x, np.float32).astype(ml_dtypes.bfloat16).astype(np.float64), axis, -1)
    blocks = v.reshape(v.shape[:-1] + (-1, 32))
    amax = np.abs(blocks).max(-1, keepdims=True)
    byte = np.maximum(np.where(amax > 0, np.frexp(amax)[1] - 1 + 127, 0) - down, 1)
    scale = np.exp2(byte - 127.0)
    codes = (blocks / scale).astype(np.float32).astype(dtype).astype(np.float64)
    return np.moveaxis((codes * scale).reshape(v.shape), -1, axis)


WIDE = False


def mx_kscale(k):
    if not WIDE:
        return np.ones(k)
    levels = np.array([10, -10, 5, -5, 0])
    if k % 512:
        return np.exp2(np.random.permutation(np.resize(levels, k // 32))).repeat(32)
    a = np.empty((k // 512, 16))
    for p in range(k // 512):
        a[p, :8] = np.random.permutation(np.resize(levels, 8))
        for g in range(8):
            far = levels[np.abs(levels - a[p, g]) >= 10]
            a[p, g + 8] = far[np.random.randint(len(far))]
    return np.exp2(a.ravel()).repeat(32)


def f64(x):
    return np.asarray(x).astype(np.float64)


def striped(idx):
    return np.tile(idx.reshape(-1, 16).T, (8, 1)).astype(np.uint16)


def unstriped(offs):
    return offs[:16].T.reshape(-1).astype(np.int64)


def pack_weight(w):
    k, n = w.shape
    w = f64(np.asarray(w, np.float32).astype(ml_dtypes.bfloat16)).reshape(k // 32, 32, n)
    amax = np.abs(w).max(1)
    byte = np.clip(np.where(amax > 0, np.frexp(amax)[1] - 1 + 127 - 7, 1), 1, 254)
    scaled = (w * np.exp2(127.0 - byte)[:, None, :]).reshape(k, n).astype(np.float32)
    words = np.ascontiguousarray(scaled.reshape(k // 512, 128, 4, n).transpose(0, 1, 3, 2)).astype(ml_dtypes.float8_e4m3fn).view(np.uint8)
    return words, np.ascontiguousarray(byte.astype(np.uint8).reshape(k // 512, 16, n))


def unpack_weight(words, scales):
    g, p, n, _ = words.shape
    vals = np.ascontiguousarray(words).view(ml_dtypes.float8_e4m3fn).astype(np.float64) * np.repeat(np.exp2(scales.astype(np.float64) - 127.0), 8, axis=1)[..., None]
    return vals.transpose(0, 1, 3, 2).reshape(g * 512, n)


def relu(v):
    return np.maximum(v, 0.0)


K, T, D, N = 512, 1024, 4, 128
P = 2 ** 7


def setup_inputs():
    n = np.random.standard_normal
    s = mx_kscale(K)[:, None]
    packed_xT = pack_weight(n((K, T)) * s)
    return {
        "x_words": packed_xT[0],
        "x_scales": packed_xT[1],
        "w1": (n((K, N)) / np.sqrt(K) / s).astype(np.float32),
        "score": np.tile(np.random.standard_normal((D, 1, T)), (1, P, 1)).astype(np.float32),
        "pos1": striped(np.random.permutation(T)),
        "pos2": striped(np.random.permutation(T)),
        "pos3": striped(np.random.permutation(T)),
        "pos4": striped(np.random.permutation(T)),
    }


def reference(x_words, x_scales, w1, score, pos1, pos2, pos3, pos4):
    xq = unpack_weight(x_words, x_scales)
    y = mxq(f64(w1), 0, "e4m3").T @ xq
    e0 = np.exp(f64(score)[0, :1])
    e1 = np.exp(f64(score)[1, :1])
    e2 = np.exp(f64(score)[2, :1])
    e3 = np.exp(f64(score)[3, :1])
    num = y[:, unstriped(pos1)] * e0 + y[:, unstriped(pos2)] * e1 + y[:, unstriped(pos3)] * e2 + y[:, unstriped(pos4)] * e3
    den = e0 + e1 + e2 + e3
    return relu(num / den)

@@ -1,0 +1,139 @@
+from contextlib import ExitStack
+
+import concourse.mybir as mybir
+from concourse.masks import make_identity
+
+F32 = mybir.dt.float32
+BF16 = mybir.dt.bfloat16
+I32 = mybir.dt.int32
+U32 = mybir.dt.uint32
+U16 = mybir.dt.uint16
+U8 = mybir.dt.uint8
+FP8X4 = mybir.dt.float8_e4m3fn_x4
+ALU = mybir.AluOpType
+ACT = mybir.ActivationFunctionType
+AXIS_X = mybir.AxisListType.X
+
+P = 128
+K, T, D, M = 512, 1024, 4, 128
+PACK = 4
+BLOCKS = T // P
+FLOPS = 2 * K * M * T
+BYTES = K * T + (K // 32) * T + 4 * K * M + 4 * D * T + D * 2 * P * (T // 16) + 4 * M * T
+X_LOAD = 1024
+N_PASS = 256
+CHUNKS = (2, 2, 2, 1, 1)
+
+
+def tile_picked_wgatv_relu_l_kernel(tc, x_words, x_scales, w1, score, pos1, pos2, pos3, pos4, out):
+    nc = tc.nc
+    with ExitStack() as ctx:
+        keep = ctx.enter_context(tc.tile_pool(name="keep", bufs=1))
+        ring = ctx.enter_context(tc.tile_pool(name="ring", bufs=8))
+        turn = ctx.enter_context(tc.psum_pool(name="turn", bufs=2))
+        sums = ctx.enter_context(tc.psum_pool(name="sums", bufs=4))
+
+        x_plane = keep.tile([P, T], U8, align_bytes=64)
+        nc.gpsimd.memset(x_plane[:].bitcast(I32), 0)
+        score_rows = keep.tile([P, 32], F32, align_bytes=64)
+        pieces = score.rearrange("d r (b n) -> (d r b) n", n=P)
+        nc.sync.dma_start(out=score_rows[:], in_=pieces[0 : D * P * BLOCKS : 129, :].rearrange("j (q a) -> q j a", a=32))
+        w_raw = keep.tile([P, PACK, M], F32)
+        nc.sync.dma_start(out=w_raw[:], in_=w1.rearrange("(p j) m -> p j m", j=PACK))
+        scale_rows = x_scales[0].bitcast(I32)
+        for q in range(4):
+            nc.sync.dma_start(out=x_plane[32 * q : 32 * q + 4, :].bitcast(I32), in_=scale_rows[4 * q : 4 * q + 4, :])
+        words = x_words[0].rearrange("p n t -> p (n t)").bitcast(I32)
+        x_codes = []
+        for h in range(T // X_LOAD):
+            codes = keep.tile([P, X_LOAD], U32, align_bytes=64, name=f"x_codes{h}")
+            nc.sync.dma_start(out=codes[:].bitcast(I32), in_=words[:, h * X_LOAD : (h + 1) * X_LOAD])
+            x_codes.append(codes)
+        lists = []
+        for d, pos in enumerate((pos1, pos2, pos3, pos4)):
+            offsets = keep.tile([P, T // 16], U16, name=f"offsets{d}")
+            nc.sync.dma_start(offsets[:], pos)
+            lists.append(offsets)
+
+        ident = keep.tile([P, P], F32)
+        make_identity(nc, ident[:])
+
+        score_t = keep.tile([P, 32], F32, align_bytes=64)
+        nc.vector.transpose(out=score_t[:], in_=score_rows[:])
+        s = score_t[:].rearrange("p (d b) -> p b d", d=D)
+        top = keep.tile([P, BLOCKS], F32)
+        nc.vector.tensor_reduce(out=top[:], in_=s, axis=AXIS_X, op=ALU.max)
+        shifted = keep.tile([P, BLOCKS, D], F32)
+        nc.vector.tensor_tensor(out=shifted[:], in0=s, in1=top[:].unsqueeze(2).to_broadcast([P, BLOCKS, D]), op=ALU.subtract)
+        fetched_all = keep.tile([P, D, BLOCKS, P], F32)
+        e = fetched_all[:, :, :, 0].rearrange("p d b -> p b d")
+        nc.scalar.activation(out=e, in_=shifted[:], func=ACT.Exp)
+        den = keep.tile([P, BLOCKS], F32)
+        nc.vector.tensor_reduce(out=den[:], in_=e, axis=AXIS_X, op=ALU.add)
+        inv = keep.tile([P, BLOCKS], F32)
+        nc.vector.reciprocal(out=inv[:], in_=den[:])
+        weight = keep.tile([P, BLOCKS, D], F32)
+        nc.vector.tensor_tensor(out=weight[:], in0=e, in1=inv[:].unsqueeze(2).to_broadcast([P, BLOCKS, D]), op=ALU.mult)
+
+        w_grouped = keep.tile([P, M, PACK], BF16, align_bytes=64)
+        nc.vector.tensor_copy(out=w_grouped[:], in_=w_raw[:].rearrange("p j m -> p m j"))
+        w_codes = keep.tile([P, M], U32, align_bytes=64)
+        w_plane = keep.tile([P, M], U8, align_bytes=64)
+        nc.vector.quantize_mx(out=w_codes[:].bitcast(FP8X4), scales=w_plane[:], in_=w_grouped[:].rearrange("p m j -> p (m j)"))
+
+        y = keep.tile([P, T], F32)
+        for c in range(T // N_PASS):
+            cols = slice(c * N_PASS, (c + 1) * N_PASS)
+            h, start = divmod(c * N_PASS, X_LOAD)
+            acc = sums.tile([P, N_PASS], F32, tag="sum")
+            nc.tensor.matmul_mx(
+                out=acc[:],
+                lhsT=w_codes[:].bitcast(FP8X4),
+                lhsT_scale=w_plane[:],
+                rhs=x_codes[h][:, start : start + N_PASS].bitcast(FP8X4),
+                rhs_scale=x_plane[:, cols],
+                start=True,
+                stop=True,
+            )
+            if c % 2 == 0:
+                nc.scalar.copy(out=y[:, cols], in_=acc[:])
+            else:
+                nc.vector.tensor_copy(out=y[:, cols], in_=acc[:])
+
+        steps = []
+        first = 0
+        for blocks in CHUNKS:
+            steps.extend((first, blocks, d) for d in range(D))
+            first = first + blocks
+        totals = {}
+
+        def fetch_and_scale(first, blocks, d):
+            entries = slice(first * P // 16, (first + blocks) * P // 16)
+            fetched = fetched_all[:, d, first : first + blocks, :]
+            nc.vector.tensor_copy(fetched.rearrange("p b n -> p (b n)"), y[:].indirect(lists[d][:, entries]))
+            turned = turn.tile([P, blocks, P], F32, tag="turn")
+            for i in range(blocks):
+                nc.tensor.transpose(turned[:, i, :], fetched[:, i, :], ident[:])
+            scaled = ring.tile([P, blocks, P], F32, tag="scaled")
+            for i in range(blocks):
+                nc.scalar.activation(out=scaled[:, i, :], in_=turned[:, i, :], func=ACT.Copy, scale=weight[:, first + i, d : d + 1])
+            return scaled
+
+        def add_up(first, blocks, d, scaled):
+            for i in range(blocks):
+                if d == 0:
+                    totals[first + i] = sums.tile([P, P], F32, tag="sum", name=f"total{first + i}")
+                nc.tensor.matmul(totals[first + i][:], lhsT=scaled[:, i, :], rhs=ident[:], is_transpose=True, start=(d == 0), stop=(d == D - 1))
+            if d == D - 1:
+                result = ring.tile([P, blocks, P], F32, tag="result")
+                for i in range(blocks):
+                    nc.scalar.activation(out=result[:, i, :], in_=totals[first + i][:], func=ACT.Relu)
+                nc.sync.dma_start(out=out[:, first * P : (first + blocks) * P], in_=result[:].rearrange("p b n -> p (b n)"))
+
+        waiting = None
+        for step in steps:
+            scaled = fetch_and_scale(*step)
+            if waiting is not None:
+                add_up(*waiting)
+            waiting = (*step, scaled)
+        add_up(*waiting)

@@ -1,7 +1,6 @@
 from contextlib import ExitStack
 
 import concourse.mybir as mybir
-from concourse.masks import make_identity
 
 F32 = mybir.dt.float32
 BF16 = mybir.dt.bfloat16
@@ -20,9 +19,10 @@ PACK = 4
 BLOCKS = T // P
 FLOPS = 2 * K * M * T
 BYTES = K * T + (K // 32) * T + 4 * K * M + 4 * D * T + D * 2 * P * (T // 16) + 4 * M * T
-X_LOAD = 1024
-N_PASS = 256
-CHUNKS = (2, 2, 2, 1, 1)
+X_LOAD = 512
+CHUNKS = (3, 2)
+LATE = 3
+PASSES = (256, 256, 256, 128, 128)
 
 
 def tile_picked_wgatv_relu_l_kernel(tc, x_words, x_scales, w1, score, pos1, pos2, pos3, pos4, out):
@@ -30,11 +30,16 @@ def tile_picked_wgatv_relu_l_kernel(tc, x_words, x_scales, w1, score, pos1, pos2
     with ExitStack() as ctx:
         keep = ctx.enter_context(tc.tile_pool(name="keep", bufs=1))
         ring = ctx.enter_context(tc.tile_pool(name="ring", bufs=8))
-        turn = ctx.enter_context(tc.psum_pool(name="turn", bufs=2))
-        sums = ctx.enter_context(tc.psum_pool(name="sums", bufs=4))
+        spread = ctx.enter_context(tc.psum_pool(name="spread", bufs=3))
+        back = ctx.enter_context(tc.psum_pool(name="back", bufs=1))
+        sums = ctx.enter_context(tc.psum_pool(name="sums", bufs=1))
 
+        ident = keep.tile([P, P], F32)
+        zeros = keep.tile([P, P], F32, align_bytes=64, tag="first")
+        nc.gpsimd.memset(zeros[:], 0.0)
+        nc.gpsimd.affine_select(out=ident[:], in_=zeros[:], compare_op=ALU.not_equal, fill=1.0, base=0, pattern=[[-1, P]], channel_multiplier=1)
         x_plane = keep.tile([P, T], U8, align_bytes=64)
-        nc.gpsimd.memset(x_plane[:].bitcast(I32), 0)
+        nc.vector.memset(x_plane[:].bitcast(I32), 0)
         score_rows = keep.tile([P, 32], F32, align_bytes=64)
         pieces = score.rearrange("d r (b n) -> (d r b) n", n=P)
         nc.sync.dma_start(out=score_rows[:], in_=pieces[0 : D * P * BLOCKS : 129, :].rearrange("j (q a) -> q j a", a=32))
@@ -55,85 +60,131 @@ def tile_picked_wgatv_relu_l_kernel(tc, x_words, x_scales, w1, score, pos1, pos2
             nc.sync.dma_start(offsets[:], pos)
             lists.append(offsets)
 
-        ident = keep.tile([P, P], F32)
-        make_identity(nc, ident[:])
 
-        score_t = keep.tile([P, 32], F32, align_bytes=64)
+        w_grouped = keep.tile([P, M, PACK], BF16, align_bytes=64)
+        nc.scalar.copy(out=w_grouped[:].rearrange("p (c i) j -> p c j i", i=4), in_=w_raw[:].rearrange("p j (c i) -> p c j i", i=4))
+        score_t = keep.tile([P, 32], F32, align_bytes=64, tag="first")
         nc.vector.transpose(out=score_t[:], in_=score_rows[:])
         s = score_t[:].rearrange("p (d b) -> p b d", d=D)
         top = keep.tile([P, BLOCKS], F32)
         nc.vector.tensor_reduce(out=top[:], in_=s, axis=AXIS_X, op=ALU.max)
         shifted = keep.tile([P, BLOCKS, D], F32)
         nc.vector.tensor_tensor(out=shifted[:], in0=s, in1=top[:].unsqueeze(2).to_broadcast([P, BLOCKS, D]), op=ALU.subtract)
-        fetched_all = keep.tile([P, D, BLOCKS, P], F32)
-        e = fetched_all[:, :, :, 0].rearrange("p d b -> p b d")
-        nc.scalar.activation(out=e, in_=shifted[:], func=ACT.Exp)
-        den = keep.tile([P, BLOCKS], F32)
-        nc.vector.tensor_reduce(out=den[:], in_=e, axis=AXIS_X, op=ALU.add)
-        inv = keep.tile([P, BLOCKS], F32)
-        nc.vector.reciprocal(out=inv[:], in_=den[:])
-        weight = keep.tile([P, BLOCKS, D], F32)
-        nc.vector.tensor_tensor(out=weight[:], in0=e, in1=inv[:].unsqueeze(2).to_broadcast([P, BLOCKS, D]), op=ALU.mult)
 
-        w_grouped = keep.tile([P, M, PACK], BF16, align_bytes=64)
-        nc.vector.tensor_copy(out=w_grouped[:], in_=w_raw[:].rearrange("p j m -> p m j"))
-        w_codes = keep.tile([P, M], U32, align_bytes=64)
+        late = BLOCKS - LATE
+        steps = [(late, LATE, d) for d in range(D - 1)]
+        first = 0
+        for blocks in CHUNKS:
+            steps.extend((first, blocks, d) for d in range(D))
+            first = first + blocks
+        pairs = [(first + i, d) for first, blocks, d in steps for i in range(blocks)]
+        plain = len(pairs)
+        factor = keep.tile([P, BLOCKS * D, P], F32)
+        weight = keep.tile([P, LATE], F32)
+
+        def column(j):
+            if j >= plain:
+                return weight[:, j - plain : j - plain + 1]
+            b, d = pairs[j]
+            return shifted[:, b, d : d + 1]
+
+        def spread_rows(start):
+            rows = spread.tile([P, D, P], F32, tag="rows")
+            for i in range(D):
+                nc.tensor.transpose(rows[:, i, :], column(start + i).to_broadcast([P, P]), ident[:])
+            cut = min(D, plain - start)
+            nc.scalar.activation(out=factor[:, start : start + cut, :], in_=rows[:, 0:cut, :], func=ACT.Exp)
+            if cut < D:
+                nc.scalar.copy(out=factor[:, start + cut : start + D, :], in_=rows[:, cut:D, :])
+
+        e = keep.tile([P, BLOCKS, D], F32, tag="window")
+        nc.scalar.activation(out=e[:], in_=shifted[:], func=ACT.Exp)
+        spread_rows(0)
+
+        w_codes = keep.tile([P, M], U32, align_bytes=64, tag="first")
         w_plane = keep.tile([P, M], U8, align_bytes=64)
         nc.vector.quantize_mx(out=w_codes[:].bitcast(FP8X4), scales=w_plane[:], in_=w_grouped[:].rearrange("p m j -> p (m j)"))
 
-        y = keep.tile([P, T], F32)
-        for c in range(T // N_PASS):
-            cols = slice(c * N_PASS, (c + 1) * N_PASS)
-            h, start = divmod(c * N_PASS, X_LOAD)
-            acc = sums.tile([P, N_PASS], F32, tag="sum")
+        den = keep.tile([P, BLOCKS], F32)
+        nc.vector.tensor_reduce(out=den[:], in_=e[:], axis=AXIS_X, op=ALU.add)
+        inv = keep.tile([P, BLOCKS], F32)
+        nc.vector.reciprocal(out=inv[:], in_=den[:])
+        nc.vector.tensor_tensor(out=weight[:], in0=e[:, late:, D - 1], in1=inv[:, late:], op=ALU.mult)
+
+        y = keep.tile([P, T], F32, tag="window")
+        homes = [(spread, "rows"), (sums, "sum0"), (sums, "sum1"), (sums, "sum2"), (spread, "rows")]
+        done = 0
+        for c, width in enumerate(PASSES):
+            cols = slice(done, done + width)
+            h, start = divmod(done, X_LOAD)
+            pool, tag = homes[c]
+            acc = pool.tile([P, width], F32, tag=tag)
             nc.tensor.matmul_mx(
                 out=acc[:],
                 lhsT=w_codes[:].bitcast(FP8X4),
                 lhsT_scale=w_plane[:],
-                rhs=x_codes[h][:, start : start + N_PASS].bitcast(FP8X4),
+                rhs=x_codes[h][:, start : start + width].bitcast(FP8X4),
                 rhs_scale=x_plane[:, cols],
                 start=True,
                 stop=True,
             )
             if c % 2 == 0:
-                nc.scalar.copy(out=y[:, cols], in_=acc[:])
-            else:
                 nc.vector.tensor_copy(out=y[:, cols], in_=acc[:])
+            else:
+                nc.scalar.copy(out=y[:, cols], in_=acc[:])
+            done = done + width
 
-        steps = []
-        first = 0
-        for blocks in CHUNKS:
-            steps.extend((first, blocks, d) for d in range(D))
-            first = first + blocks
-        totals = {}
+        for start in range(D, BLOCKS * D, D):
+            spread_rows(start)
 
-        def fetch_and_scale(first, blocks, d):
+        terms = keep.tile([P, BLOCKS * D, P], F32)
+
+        def fetch(first, blocks, d, slot):
             entries = slice(first * P // 16, (first + blocks) * P // 16)
-            fetched = fetched_all[:, d, first : first + blocks, :]
-            nc.vector.tensor_copy(fetched.rearrange("p b n -> p (b n)"), y[:].indirect(lists[d][:, entries]))
-            turned = turn.tile([P, blocks, P], F32, tag="turn")
-            for i in range(blocks):
-                nc.tensor.transpose(turned[:, i, :], fetched[:, i, :], ident[:])
-            scaled = ring.tile([P, blocks, P], F32, tag="scaled")
-            for i in range(blocks):
-                nc.scalar.activation(out=scaled[:, i, :], in_=turned[:, i, :], func=ACT.Copy, scale=weight[:, first + i, d : d + 1])
-            return scaled
+            nc.vector.tensor_tensor(
+                terms[:, slot : slot + blocks, :].rearrange("p b n -> p (b n)"),
+                y[:].indirect(lists[d][:, entries]),
+                factor[:, slot : slot + blocks, :].rearrange("p b n -> p (b n)"),
+                ALU.mult,
+            )
 
-        def add_up(first, blocks, d, scaled):
+        def turn_back(first, blocks, totals, func, tag):
+            turned = ring.tile([P, blocks, P], F32, tag="turned")
             for i in range(blocks):
-                if d == 0:
-                    totals[first + i] = sums.tile([P, P], F32, tag="sum", name=f"total{first + i}")
-                nc.tensor.matmul(totals[first + i][:], lhsT=scaled[:, i, :], rhs=ident[:], is_transpose=True, start=(d == 0), stop=(d == D - 1))
-            if d == D - 1:
+                nc.scalar.activation(out=turned[:, i, :], in_=totals[i][:], func=func, scale=inv[:, first + i : first + i + 1])
+            upright = back.tile([P, blocks, P], F32, tag=tag)
+            for i in range(blocks):
+                nc.tensor.transpose(upright[:, i, :], turned[:, i, :], ident[:])
+            return upright
+
+        slot = 0
+        for first, blocks, d in steps:
+            closing = D - 2 if first == late else D - 1
+            if d == 0:
+                totals = [sums.tile([P, P], F32, tag=f"sum{i}", name=f"total{first + i}") for i in range(blocks)]
+            by_block = first + blocks == late and d == closing
+            if not by_block:
+                fetch(first, blocks, d, slot)
+            for i in range(blocks):
+                if by_block:
+                    fetch(first + i, 1, d, slot + i)
+                nc.tensor.matmul(totals[i][:], lhsT=terms[:, slot + i, :], rhs=ident[:], is_transpose=True, start=(d == 0), stop=(d == closing))
+            slot = slot + blocks
+            if d == closing and first == late:
+                partial = turn_back(first, blocks, totals, ACT.Copy, "partial")
+            elif d == closing:
+                upright = turn_back(first, blocks, totals, ACT.Relu, "upright")
                 result = ring.tile([P, blocks, P], F32, tag="result")
-                for i in range(blocks):
-                    nc.scalar.activation(out=result[:, i, :], in_=totals[first + i][:], func=ACT.Relu)
-                nc.sync.dma_start(out=out[:, first * P : (first + blocks) * P], in_=result[:].rearrange("p b n -> p (b n)"))
+                nc.scalar.copy(out=result[:], in_=upright[:])
+                nc.scalar.dma_start(out=out[:, first * P : (first + blocks) * P], in_=result[:].rearrange("p b n -> p (b n)"))
 
-        waiting = None
-        for step in steps:
-            scaled = fetch_and_scale(*step)
-            if waiting is not None:
-                add_up(*waiting)
-            waiting = (*step, scaled)
-        add_up(*waiting)
+        summed = keep.tile([P, LATE, P], F32)
+        clipped = keep.tile([P, LATE, P], F32)
+        for i in range(LATE):
+            fetch(late + i, 1, D - 1, slot + i)
+        for i in range(LATE):
+            nc.vector.tensor_tensor(summed[:, i, :], partial[:, i, :], terms[:, slot + i, :], ALU.add)
+        for i in range(LATE):
+            nc.vector.tensor_scalar(clipped[:, i, :], summed[:, i, :], 0.0, None, ALU.max)
+        nc.sync.dma_start(out=out[:, late * P : T - P], in_=clipped[:, 0 : LATE - 1, :].rearrange("p b n -> p (b n)"))
+        nc.sync.dma_start(out=out[:, T - P :], in_=clipped[:, LATE - 1, :])

@@ -14,40 +14,47 @@ ACT = mybir.ActivationFunctionType
 AXIS_X = mybir.AxisListType.X
 
 P = 128
+QUAD = 32
 K, T, D, M = 512, 1024, 4, 128
 PACK = 4
 BLOCKS = T // P
 FLOPS = 2 * K * M * T
 BYTES = K * T + (K // 32) * T + 4 * K * M + 4 * D * T + D * 2 * P * (T // 16) + 4 * M * T
+
 X_LOAD = 512
-CHUNKS = (3, 2)
-LATE = 3
 PASSES = (256, 256, 256, 128, 128)
+LATE = 3
+CHUNKS = (3, 2)
 
 
 def tile_picked_wgatv_relu_l_kernel(tc, x_words, x_scales, w1, score, pos1, pos2, pos3, pos4, out):
     nc = tc.nc
     with ExitStack() as ctx:
         keep = ctx.enter_context(tc.tile_pool(name="keep", bufs=1))
-        ring = ctx.enter_context(tc.tile_pool(name="ring", bufs=8))
+        ring = ctx.enter_context(tc.tile_pool(name="ring", bufs=4))
         spread = ctx.enter_context(tc.psum_pool(name="spread", bufs=3))
-        back = ctx.enter_context(tc.psum_pool(name="back", bufs=1))
-        sums = ctx.enter_context(tc.psum_pool(name="sums", bufs=1))
+        banks = ctx.enter_context(tc.psum_pool(name="banks", bufs=1))
 
         ident = keep.tile([P, P], F32)
-        zeros = keep.tile([P, P], F32, align_bytes=64, tag="first")
+        zeros = keep.tile([P, P], F32, align_bytes=64, tag="head")
         nc.gpsimd.memset(zeros[:], 0.0)
-        nc.gpsimd.affine_select(out=ident[:], in_=zeros[:], compare_op=ALU.not_equal, fill=1.0, base=0, pattern=[[-1, P]], channel_multiplier=1)
-        x_plane = keep.tile([P, T], U8, align_bytes=64)
-        nc.vector.memset(x_plane[:].bitcast(I32), 0)
-        score_rows = keep.tile([P, 32], F32, align_bytes=64)
+        nc.gpsimd.affine_select(
+            out=ident[:], in_=zeros[:], compare_op=ALU.not_equal, fill=1.0, base=0, pattern=[[-1, P]], channel_multiplier=1
+        )
+
+        x_scale_tile = keep.tile([P, T], U8, align_bytes=64)
+        nc.vector.memset(x_scale_tile[:].bitcast(I32), 0)
+
+        score_rows = keep.tile([P, QUAD], F32, align_bytes=64)
         pieces = score.rearrange("d r (b n) -> (d r b) n", n=P)
-        nc.sync.dma_start(out=score_rows[:], in_=pieces[0 : D * P * BLOCKS : 129, :].rearrange("j (q a) -> q j a", a=32))
+        piece_step = P + 1
+        nc.sync.dma_start(out=score_rows[:], in_=pieces[0 : D * P * BLOCKS : piece_step, :].rearrange("j (q a) -> q j a", a=QUAD))
+
         w_raw = keep.tile([P, PACK, M], F32)
-        nc.sync.dma_start(out=w_raw[:], in_=w1.rearrange("(p j) m -> p j m", j=PACK))
+        nc.sync.dma_start(out=w_raw[:], in_=w1.rearrange("(p t) m -> p t m", t=PACK))
         scale_rows = x_scales[0].bitcast(I32)
-        for q in range(4):
-            nc.sync.dma_start(out=x_plane[32 * q : 32 * q + 4, :].bitcast(I32), in_=scale_rows[4 * q : 4 * q + 4, :])
+        for q in range(P // QUAD):
+            nc.sync.dma_start(out=x_scale_tile[QUAD * q : QUAD * q + 4, :].bitcast(I32), in_=scale_rows[4 * q : 4 * q + 4, :])
         words = x_words[0].rearrange("p n t -> p (n t)").bitcast(I32)
         x_codes = []
         for h in range(T // X_LOAD):
@@ -60,16 +67,18 @@ def tile_picked_wgatv_relu_l_kernel(tc, x_words, x_scales, w1, score, pos1, pos2
             nc.sync.dma_start(offsets[:], pos)
             lists.append(offsets)
 
-
         w_grouped = keep.tile([P, M, PACK], BF16, align_bytes=64)
-        nc.scalar.copy(out=w_grouped[:].rearrange("p (c i) j -> p c j i", i=4), in_=w_raw[:].rearrange("p j (c i) -> p c j i", i=4))
-        score_t = keep.tile([P, 32], F32, align_bytes=64, tag="first")
+        nc.scalar.copy(
+            out=w_grouped[:].rearrange("p (c i) t -> p c t i", i=4), in_=w_raw[:].rearrange("p t (c i) -> p c t i", i=4)
+        )
+
+        score_t = keep.tile([P, QUAD], F32, align_bytes=64, tag="head")
         nc.vector.transpose(out=score_t[:], in_=score_rows[:])
-        s = score_t[:].rearrange("p (d b) -> p b d", d=D)
+        by_target = score_t[:].rearrange("p (d b) -> p b d", d=D)
         top = keep.tile([P, BLOCKS], F32)
-        nc.vector.tensor_reduce(out=top[:], in_=s, axis=AXIS_X, op=ALU.max)
+        nc.vector.tensor_reduce(out=top[:], in_=by_target, axis=AXIS_X, op=ALU.max)
         shifted = keep.tile([P, BLOCKS, D], F32)
-        nc.vector.tensor_tensor(out=shifted[:], in0=s, in1=top[:].unsqueeze(2).to_broadcast([P, BLOCKS, D]), op=ALU.subtract)
+        nc.vector.tensor_tensor(out=shifted[:], in0=by_target, in1=top[:].unsqueeze(2).to_broadcast([P, BLOCKS, D]), op=ALU.subtract)
 
         late = BLOCKS - LATE
         steps = [(late, LATE, d) for d in range(D - 1)]
@@ -77,42 +86,39 @@ def tile_picked_wgatv_relu_l_kernel(tc, x_words, x_scales, w1, score, pos1, pos2
         for blocks in CHUNKS:
             steps.extend((first, blocks, d) for d in range(D))
             first = first + blocks
-        pairs = [(first + i, d) for first, blocks, d in steps for i in range(blocks)]
-        plain = len(pairs)
+        slots = [sum(blocks for first, blocks, d in steps[:i]) for i in range(len(steps) + 1)]
         factor = keep.tile([P, BLOCKS * D, P], F32)
-        weight = keep.tile([P, LATE], F32)
+        terms = keep.tile([P, BLOCKS * D, P], F32)
 
-        def column(j):
-            if j >= plain:
-                return weight[:, j - plain : j - plain + 1]
-            b, d = pairs[j]
-            return shifted[:, b, d : d + 1]
+        def spread_rows(columns, slot, func):
+            rows = spread.tile([P, len(columns), P], F32, tag="rows")
+            for i, column in enumerate(columns):
+                nc.tensor.transpose(rows[:, i, :], column.to_broadcast([P, P]), ident[:])
+            nc.scalar.activation(out=factor[:, slot : slot + len(columns), :], in_=rows[:], func=func)
 
-        def spread_rows(start):
-            rows = spread.tile([P, D, P], F32, tag="rows")
-            for i in range(D):
-                nc.tensor.transpose(rows[:, i, :], column(start + i).to_broadcast([P, P]), ident[:])
-            cut = min(D, plain - start)
-            nc.scalar.activation(out=factor[:, start : start + cut, :], in_=rows[:, 0:cut, :], func=ACT.Exp)
-            if cut < D:
-                nc.scalar.copy(out=factor[:, start + cut : start + D, :], in_=rows[:, cut:D, :])
+        def spread_step(index):
+            first, blocks, d = steps[index]
+            spread_rows([shifted[:, first + i, d : d + 1] for i in range(blocks)], slots[index], ACT.Exp)
 
         e = keep.tile([P, BLOCKS, D], F32, tag="window")
         nc.scalar.activation(out=e[:], in_=shifted[:], func=ACT.Exp)
-        spread_rows(0)
+        spread_step(0)
 
-        w_codes = keep.tile([P, M], U32, align_bytes=64, tag="first")
-        w_plane = keep.tile([P, M], U8, align_bytes=64)
-        nc.vector.quantize_mx(out=w_codes[:].bitcast(FP8X4), scales=w_plane[:], in_=w_grouped[:].rearrange("p m j -> p (m j)"))
+        w_codes = keep.tile([P, M], U32, align_bytes=64, tag="head")
+        w_scale_tile = keep.tile([P, M], U8, align_bytes=64)
+        nc.vector.quantize_mx(
+            out=w_codes[:].bitcast(FP8X4), scales=w_scale_tile[:], in_=w_grouped[:].rearrange("p m t -> p (m t)")
+        )
 
         den = keep.tile([P, BLOCKS], F32)
         nc.vector.tensor_reduce(out=den[:], in_=e[:], axis=AXIS_X, op=ALU.add)
         inv = keep.tile([P, BLOCKS], F32)
         nc.vector.reciprocal(out=inv[:], in_=den[:])
-        nc.vector.tensor_tensor(out=weight[:], in0=e[:, late:, D - 1], in1=inv[:, late:], op=ALU.mult)
+        last_weight = keep.tile([P, LATE], F32)
+        nc.vector.tensor_tensor(out=last_weight[:], in0=e[:, late:, D - 1], in1=inv[:, late:], op=ALU.mult)
 
         y = keep.tile([P, T], F32, tag="window")
-        homes = [(spread, "rows"), (sums, "sum0"), (sums, "sum1"), (sums, "sum2"), (spread, "rows")]
+        homes = [(spread, "rows"), (banks, "sum0"), (banks, "sum1"), (banks, "sum2"), (spread, "rows")]
         done = 0
         for c, width in enumerate(PASSES):
             cols = slice(done, done + width)
@@ -122,9 +128,9 @@ def tile_picked_wgatv_relu_l_kernel(tc, x_words, x_scales, w1, score, pos1, pos2
             nc.tensor.matmul_mx(
                 out=acc[:],
                 lhsT=w_codes[:].bitcast(FP8X4),
-                lhsT_scale=w_plane[:],
+                lhsT_scale=w_scale_tile[:],
                 rhs=x_codes[h][:, start : start + width].bitcast(FP8X4),
-                rhs_scale=x_plane[:, cols],
+                rhs_scale=x_scale_tile[:, cols],
                 start=True,
                 stop=True,
             )
@@ -134,10 +140,9 @@ def tile_picked_wgatv_relu_l_kernel(tc, x_words, x_scales, w1, score, pos1, pos2
                 nc.scalar.copy(out=y[:, cols], in_=acc[:])
             done = done + width
 
-        for start in range(D, BLOCKS * D, D):
-            spread_rows(start)
-
-        terms = keep.tile([P, BLOCKS * D, P], F32)
+        for index in range(1, len(steps)):
+            spread_step(index)
+        spread_rows([last_weight[:, i : i + 1] for i in range(LATE)], slots[-1], ACT.Copy)
 
         def fetch(first, blocks, d, slot):
             entries = slice(first * P // 16, (first + blocks) * P // 16)
@@ -148,42 +153,44 @@ def tile_picked_wgatv_relu_l_kernel(tc, x_words, x_scales, w1, score, pos1, pos2
                 ALU.mult,
             )
 
-        def turn_back(first, blocks, totals, func, tag):
-            turned = ring.tile([P, blocks, P], F32, tag="turned")
-            for i in range(blocks):
-                nc.scalar.activation(out=turned[:, i, :], in_=totals[i][:], func=func, scale=inv[:, first + i : first + i + 1])
-            upright = back.tile([P, blocks, P], F32, tag=tag)
-            for i in range(blocks):
+        def turn_back(first, totals, func, upright):
+            turned = ring.tile([P, len(totals), P], F32, tag="turned")
+            for i, total in enumerate(totals):
+                nc.scalar.activation(out=turned[:, i, :], in_=total[:], func=func, scale=inv[:, first + i : first + i + 1])
+            for i in range(len(totals)):
                 nc.tensor.transpose(upright[:, i, :], turned[:, i, :], ident[:])
-            return upright
 
-        slot = 0
-        for first, blocks, d in steps:
+        for (first, blocks, d), slot in zip(steps, slots):
             closing = D - 2 if first == late else D - 1
-            if d == 0:
-                totals = [sums.tile([P, P], F32, tag=f"sum{i}", name=f"total{first + i}") for i in range(blocks)]
             by_block = first + blocks == late and d == closing
+            if d == 0:
+                totals = [banks.tile([P, P], F32, tag=f"sum{i}", name=f"total{first + i}") for i in range(blocks)]
             if not by_block:
                 fetch(first, blocks, d, slot)
             for i in range(blocks):
                 if by_block:
                     fetch(first + i, 1, d, slot + i)
-                nc.tensor.matmul(totals[i][:], lhsT=terms[:, slot + i, :], rhs=ident[:], is_transpose=True, start=(d == 0), stop=(d == closing))
-            slot = slot + blocks
+                nc.tensor.matmul(
+                    totals[i][:], lhsT=terms[:, slot + i, :], rhs=ident[:], is_transpose=True, start=(d == 0), stop=(d == closing)
+                )
             if d == closing and first == late:
-                partial = turn_back(first, blocks, totals, ACT.Copy, "partial")
+                partial = banks.tile([P, LATE, P], F32, tag="partial")
+                turn_back(first, totals, ACT.Copy, partial)
             elif d == closing:
-                upright = turn_back(first, blocks, totals, ACT.Relu, "upright")
                 result = ring.tile([P, blocks, P], F32, tag="result")
-                nc.scalar.copy(out=result[:], in_=upright[:])
+                groups = [(i, 1) for i in range(blocks)] if by_block else [(0, blocks)]
+                for i, count in groups:
+                    upright = banks.tile([P, count, P], F32, tag=("upright", "sum2")[i])
+                    turn_back(first + i, totals[i : i + count], ACT.Relu, upright)
+                    nc.scalar.copy(out=result[:, i : i + count, :], in_=upright[:])
                 nc.scalar.dma_start(out=out[:, first * P : (first + blocks) * P], in_=result[:].rearrange("p b n -> p (b n)"))
 
         summed = keep.tile([P, LATE, P], F32)
         clipped = keep.tile([P, LATE, P], F32)
         for i in range(LATE):
-            fetch(late + i, 1, D - 1, slot + i)
+            fetch(late + i, 1, D - 1, slots[-1] + i)
         for i in range(LATE):
-            nc.vector.tensor_tensor(summed[:, i, :], partial[:, i, :], terms[:, slot + i, :], ALU.add)
+            nc.vector.tensor_tensor(summed[:, i, :], partial[:, i, :], terms[:, slots[-1] + i, :], ALU.add)
         for i in range(LATE):
             nc.vector.tensor_scalar(clipped[:, i, :], summed[:, i, :], 0.0, None, ALU.max)
         nc.sync.dma_start(out=out[:, late * P : T - P], in_=clipped[:, 0 : LATE - 1, :].rearrange("p b n -> p (b n)"))

from contextlib import ExitStack

import concourse.mybir as mybir

F32 = mybir.dt.float32
BF16 = mybir.dt.bfloat16
I32 = mybir.dt.int32
U32 = mybir.dt.uint32
U16 = mybir.dt.uint16
U8 = mybir.dt.uint8
FP8X4 = mybir.dt.float8_e4m3fn_x4
ALU = mybir.AluOpType
ACT = mybir.ActivationFunctionType
AXIS_X = mybir.AxisListType.X

P = 128
QUAD = 32
K, T, D, M = 512, 1024, 4, 128
PACK = 4
BLOCKS = T // P
FLOPS = 2 * K * M * T
BYTES = K * T + (K // 32) * T + 4 * K * M + 4 * D * T + D * 2 * P * (T // 16) + 4 * M * T

X_LOAD = 512
PASSES = (256, 256, 256, 128, 128)
LATE = 3
CHUNKS = (3, 2)


def tile_picked_wgatv_relu_l_kernel(tc, x_words, x_scales, w1, score, pos1, pos2, pos3, pos4, out):
    nc = tc.nc
    with ExitStack() as ctx:
        keep = ctx.enter_context(tc.tile_pool(name="keep", bufs=1))
        ring = ctx.enter_context(tc.tile_pool(name="ring", bufs=4))
        spread = ctx.enter_context(tc.psum_pool(name="spread", bufs=3))
        banks = ctx.enter_context(tc.psum_pool(name="banks", bufs=1))

        ident = keep.tile([P, P], F32)
        zeros = keep.tile([P, P], F32, align_bytes=64, tag="head")
        nc.gpsimd.memset(zeros[:], 0.0)
        nc.gpsimd.affine_select(
            out=ident[:], in_=zeros[:], compare_op=ALU.not_equal, fill=1.0, base=0, pattern=[[-1, P]], channel_multiplier=1
        )

        x_scale_tile = keep.tile([P, T], U8, align_bytes=64)
        nc.vector.memset(x_scale_tile[:].bitcast(I32), 0)

        score_rows = keep.tile([P, QUAD], F32, align_bytes=64)
        pieces = score.rearrange("d r (b n) -> (d r b) n", n=P)
        piece_step = P + 1
        nc.sync.dma_start(out=score_rows[:], in_=pieces[0 : D * P * BLOCKS : piece_step, :].rearrange("j (q a) -> q j a", a=QUAD))

        w_raw = keep.tile([P, PACK, M], F32)
        nc.sync.dma_start(out=w_raw[:], in_=w1.rearrange("(p t) m -> p t m", t=PACK))
        scale_rows = x_scales[0].bitcast(I32)
        for q in range(P // QUAD):
            nc.sync.dma_start(out=x_scale_tile[QUAD * q : QUAD * q + 4, :].bitcast(I32), in_=scale_rows[4 * q : 4 * q + 4, :])
        words = x_words[0].rearrange("p n t -> p (n t)").bitcast(I32)
        x_codes = []
        for h in range(T // X_LOAD):
            codes = keep.tile([P, X_LOAD], U32, align_bytes=64, name=f"x_codes{h}")
            nc.sync.dma_start(out=codes[:].bitcast(I32), in_=words[:, h * X_LOAD : (h + 1) * X_LOAD])
            x_codes.append(codes)
        lists = []
        for d, pos in enumerate((pos1, pos2, pos3, pos4)):
            offsets = keep.tile([P, T // 16], U16, name=f"offsets{d}")
            nc.sync.dma_start(offsets[:], pos)
            lists.append(offsets)

        w_grouped = keep.tile([P, M, PACK], BF16, align_bytes=64)
        nc.scalar.copy(
            out=w_grouped[:].rearrange("p (c i) t -> p c t i", i=4), in_=w_raw[:].rearrange("p t (c i) -> p c t i", i=4)
        )

        score_t = keep.tile([P, QUAD], F32, align_bytes=64, tag="head")
        nc.vector.transpose(out=score_t[:], in_=score_rows[:])
        by_target = score_t[:].rearrange("p (d b) -> p b d", d=D)
        top = keep.tile([P, BLOCKS], F32)
        nc.vector.tensor_reduce(out=top[:], in_=by_target, axis=AXIS_X, op=ALU.max)
        shifted = keep.tile([P, BLOCKS, D], F32)
        nc.vector.tensor_tensor(out=shifted[:], in0=by_target, in1=top[:].unsqueeze(2).to_broadcast([P, BLOCKS, D]), op=ALU.subtract)

        late = BLOCKS - LATE
        steps = [(late, LATE, d) for d in range(D - 1)]
        first = 0
        for blocks in CHUNKS:
            steps.extend((first, blocks, d) for d in range(D))
            first = first + blocks
        slots = [sum(blocks for first, blocks, d in steps[:i]) for i in range(len(steps) + 1)]
        factor = keep.tile([P, BLOCKS * D, P], F32)
        terms = keep.tile([P, BLOCKS * D, P], F32)

        def spread_rows(columns, slot, func):
            rows = spread.tile([P, len(columns), P], F32, tag="rows")
            for i, column in enumerate(columns):
                nc.tensor.transpose(rows[:, i, :], column.to_broadcast([P, P]), ident[:])
            nc.scalar.activation(out=factor[:, slot : slot + len(columns), :], in_=rows[:], func=func)

        def spread_step(index):
            first, blocks, d = steps[index]
            spread_rows([shifted[:, first + i, d : d + 1] for i in range(blocks)], slots[index], ACT.Exp)

        e = keep.tile([P, BLOCKS, D], F32, tag="window")
        nc.scalar.activation(out=e[:], in_=shifted[:], func=ACT.Exp)
        spread_step(0)

        w_codes = keep.tile([P, M], U32, align_bytes=64, tag="head")
        w_scale_tile = keep.tile([P, M], U8, align_bytes=64)
        nc.vector.quantize_mx(
            out=w_codes[:].bitcast(FP8X4), scales=w_scale_tile[:], in_=w_grouped[:].rearrange("p m t -> p (m t)")
        )

        den = keep.tile([P, BLOCKS], F32)
        nc.vector.tensor_reduce(out=den[:], in_=e[:], axis=AXIS_X, op=ALU.add)
        inv = keep.tile([P, BLOCKS], F32)
        nc.vector.reciprocal(out=inv[:], in_=den[:])
        last_weight = keep.tile([P, LATE], F32)
        nc.vector.tensor_tensor(out=last_weight[:], in0=e[:, late:, D - 1], in1=inv[:, late:], op=ALU.mult)

        y = keep.tile([P, T], F32, tag="window")
        homes = [(spread, "rows"), (banks, "sum0"), (banks, "sum1"), (banks, "sum2"), (spread, "rows")]
        done = 0
        for c, width in enumerate(PASSES):
            cols = slice(done, done + width)
            h, start = divmod(done, X_LOAD)
            pool, tag = homes[c]
            acc = pool.tile([P, width], F32, tag=tag)
            nc.tensor.matmul_mx(
                out=acc[:],
                lhsT=w_codes[:].bitcast(FP8X4),
                lhsT_scale=w_scale_tile[:],
                rhs=x_codes[h][:, start : start + width].bitcast(FP8X4),
                rhs_scale=x_scale_tile[:, cols],
                start=True,
                stop=True,
            )
            if c % 2 == 0:
                nc.vector.tensor_copy(out=y[:, cols], in_=acc[:])
            else:
                nc.scalar.copy(out=y[:, cols], in_=acc[:])
            done = done + width

        for index in range(1, len(steps)):
            spread_step(index)
        spread_rows([last_weight[:, i : i + 1] for i in range(LATE)], slots[-1], ACT.Copy)

        def fetch(first, blocks, d, slot):
            entries = slice(first * P // 16, (first + blocks) * P // 16)
            nc.vector.tensor_tensor(
                terms[:, slot : slot + blocks, :].rearrange("p b n -> p (b n)"),
                y[:].indirect(lists[d][:, entries]),
                factor[:, slot : slot + blocks, :].rearrange("p b n -> p (b n)"),
                ALU.mult,
            )

        def turn_back(first, totals, func, upright):
            turned = ring.tile([P, len(totals), P], F32, tag="turned")
            for i, total in enumerate(totals):
                nc.scalar.activation(out=turned[:, i, :], in_=total[:], func=func, scale=inv[:, first + i : first + i + 1])
            for i in range(len(totals)):
                nc.tensor.transpose(upright[:, i, :], turned[:, i, :], ident[:])

        for (first, blocks, d), slot in zip(steps, slots):
            closing = D - 2 if first == late else D - 1
            by_block = first + blocks == late and d == closing
            if d == 0:
                totals = [banks.tile([P, P], F32, tag=f"sum{i}", name=f"total{first + i}") for i in range(blocks)]
            if not by_block:
                fetch(first, blocks, d, slot)
            for i in range(blocks):
                if by_block:
                    fetch(first + i, 1, d, slot + i)
                nc.tensor.matmul(
                    totals[i][:], lhsT=terms[:, slot + i, :], rhs=ident[:], is_transpose=True, start=(d == 0), stop=(d == closing)
                )
            if d == closing and first == late:
                partial = banks.tile([P, LATE, P], F32, tag="partial")
                turn_back(first, totals, ACT.Copy, partial)
            elif d == closing:
                result = ring.tile([P, blocks, P], F32, tag="result")
                groups = [(i, 1) for i in range(blocks)] if by_block else [(0, blocks)]
                for i, count in groups:
                    upright = banks.tile([P, count, P], F32, tag=("upright", "sum2")[i])
                    turn_back(first + i, totals[i : i + count], ACT.Relu, upright)
                    nc.scalar.copy(out=result[:, i : i + count, :], in_=upright[:])
                nc.scalar.dma_start(out=out[:, first * P : (first + blocks) * P], in_=result[:].rearrange("p b n -> p (b n)"))

        summed = keep.tile([P, LATE, P], F32)
        clipped = keep.tile([P, LATE, P], F32)
        for i in range(LATE):
            fetch(late + i, 1, D - 1, slots[-1] + i)
        for i in range(LATE):
            nc.vector.tensor_tensor(summed[:, i, :], partial[:, i, :], terms[:, slots[-1] + i, :], ALU.add)
        for i in range(LATE):
            nc.vector.tensor_scalar(clipped[:, i, :], summed[:, i, :], 0.0, None, ALU.max)
        nc.sync.dma_start(out=out[:, late * P : T - P], in_=clipped[:, 0 : LATE - 1, :].rearrange("p b n -> p (b n)"))
        nc.sync.dma_start(out=out[:, T - P :], in_=clipped[:, LATE - 1, :])
